import numpy as np
import ml_dtypes


def mxq(x, axis, fmt="e4m3"):
    dtype, down = {"e4m3": (ml_dtypes.float8_e4m3fn, 7), "e5m2": (ml_dtypes.float8_e5m2, 14)}[fmt]
    v = np.moveaxis(np.asarray(x, np.float32).astype(ml_dtypes.bfloat16).astype(np.float64), axis, -1)
    blocks = v.reshape(v.shape[:-1] + (-1, 32))
    amax = np.abs(blocks).max(-1, keepdims=True)
    byte = np.maximum(np.where(amax > 0, np.frexp(amax)[1] - 1 + 127, 0) - down, 1)
    scale = np.exp2(byte - 127.0)
    codes = (blocks / scale).astype(np.float32).astype(dtype).astype(np.float64)
    return np.moveaxis((codes * scale).reshape(v.shape), -1, axis)


WIDE = False


def mx_kscale(k):
    if not WIDE:
        return np.ones(k)
    levels = np.array([10, -10, 5, -5, 0])
    if k % 512:
        return np.exp2(np.random.permutation(np.resize(levels, k // 32))).repeat(32)
    a = np.empty((k // 512, 16))
    for p in range(k // 512):
        a[p, :8] = np.random.permutation(np.resize(levels, 8))
        for g in range(8):
            far = levels[np.abs(levels - a[p, g]) >= 10]
            a[p, g + 8] = far[np.random.randint(len(far))]
    return np.exp2(a.ravel()).repeat(32)


def f64(x):
    return np.asarray(x).astype(np.float64)


def striped(idx):
    return np.tile(idx.reshape(-1, 16).T, (8, 1)).astype(np.uint16)


def unstriped(offs):
    return offs[:16].T.reshape(-1).astype(np.int64)


def pack_weight(w):
    k, n = w.shape
    w = f64(np.asarray(w, np.float32).astype(ml_dtypes.bfloat16)).reshape(k // 32, 32, n)
    amax = np.abs(w).max(1)
    byte = np.clip(np.where(amax > 0, np.frexp(amax)[1] - 1 + 127 - 7, 1), 1, 254)
    scaled = (w * np.exp2(127.0 - byte)[:, None, :]).reshape(k, n).astype(np.float32)
    words = np.ascontiguousarray(scaled.reshape(k // 512, 128, 4, n).transpose(0, 1, 3, 2)).astype(ml_dtypes.float8_e4m3fn).view(np.uint8)
    return words, np.ascontiguousarray(byte.astype(np.uint8).reshape(k // 512, 16, n))


def unpack_weight(words, scales):
    g, p, n, _ = words.shape
    vals = np.ascontiguousarray(words).view(ml_dtypes.float8_e4m3fn).astype(np.float64) * np.repeat(np.exp2(scales.astype(np.float64) - 127.0), 8, axis=1)[..., None]
    return vals.transpose(0, 1, 3, 2).reshape(g * 512, n)


K, T, E, C, N = 1024, 512, 4, 128, 128


def by_expert(wq, xq):
    return np.concatenate([wq[e].T @ xq[:, e * C:(e + 1) * C] for e in range(E)], axis=1)


def setup_inputs():
    n = np.random.standard_normal
    s = mx_kscale(K)[:, None]
    packed = [pack_weight(m) for m in n((E, K, N)) / np.sqrt(K) / s[None]]
    return {
        "xT": (n((K, T)) * s).astype(np.float32),
        "w_words": np.stack([m[0] for m in packed]),
        "w_scales": np.stack([m[1] for m in packed]),
        "offs": striped(np.random.permutation(T)[:E * C]),
    }


def reference(xT, w_words, w_scales, offs):
    idx = unstriped(offs)
    xq = mxq(f64(xT)[:, idx], 0, "e4m3")
    w = np.stack([unpack_weight(w_words[e], w_scales[e]) for e in range(E)])
    y = by_expert(w, xq)
    out = np.zeros((N, T))
    out[:, idx] = y
    return out

@@ -1,0 +1,168 @@
+import concourse.mybir as mybir
+
+FLOPS = 2 * 1024 * 128 * 512
+
+F32 = mybir.dt.float32
+BF16 = mybir.dt.bfloat16
+I32 = mybir.dt.int32
+U32 = mybir.dt.uint32
+U16 = mybir.dt.uint16
+U8 = mybir.dt.uint8
+FP8X4 = mybir.dt.float8_e4m3fn_x4
+COPY = mybir.ActivationFunctionType.Copy
+MULT = mybir.AluOpType.mult
+ADD = mybir.AluOpType.add
+
+P = 128
+T = 512
+E = 4
+C = 128
+N = 128
+PASSES = 2
+HALF = T // 2
+
+EARLY, LATE = 1, 0
+PAIR_PIECES = ((LATE, 0), (EARLY, 0), (EARLY, 1))
+PLANE_PIECE = (LATE, 1)
+
+PAIR_CASTS = (
+    (("vector", 0, 176), ("scalar", 176, 80), ("vector", 256, 88), ("scalar", 344, 40), ("vector", 384, 88), ("scalar", 472, 40)),
+    (("scalar", 0, 384), ("gpsimd", 384, 128)),
+    (("scalar", 0, 368), ("gpsimd", 368, 144)),
+)
+PLANE0_FOR_GPSIMD = 304
+
+
+def tile_routed_moe_kernel(tc, xT, w_words, w_scales, offs, out):
+    nc = tc.nc
+    with (
+        tc.tile_pool(name="keep", bufs=1) as keep,
+        tc.psum_pool(name="psum", bufs=1) as psum,
+    ):
+        lists = keep.tile([P, T // 16], U16, name="lists")
+        x_view = xT.rearrange("(g p u v) n -> g u p v n", g=PASSES, p=P, u=2, v=2)
+        raw_pairs = [keep.tile([P, 2, T], F32, name="raw_pairs%d" % i) for i in range(len(PAIR_PIECES))]
+        raw_planes = keep.tile([P, 2, T], F32, name="raw_planes")
+        first = x_view[PAIR_PIECES[0][0], PAIR_PIECES[0][1]]
+        for a, b in ((0, 256), (256, 384), (384, 512)):
+            nc.sync.dma_start(raw_pairs[0][:, :, a:b], first[:, :, a:b])
+        nc.sync.dma_start(lists[:], offs)
+        for i in range(1, len(PAIR_PIECES)):
+            nc.sync.dma_start(raw_pairs[i][:], x_view[PAIR_PIECES[i][0], PAIR_PIECES[i][1]])
+        for v in range(2):
+            nc.sync.dma_start(raw_planes[:, v, :], x_view[PLANE_PIECE[0], PLANE_PIECE[1]][:, v, :])
+
+        warm_in = keep.tile([P, 1], F32, name="warm_in")
+        warm_out = keep.tile([P, 1], F32, name="warm_out")
+        nc.vector.memset(warm_in[:], 0.0)
+        nc.scalar.copy(out=warm_out[:], in_=warm_in[:])
+
+        w_scale_sb = keep.tile([P, E * PASSES, N], U8, name="w_scale_sb", align_bytes=64)
+        nc.vector.memset(w_scale_sb[:].rearrange("p i n -> p (i n)").bitcast(I32), 0)
+        scale_rows = w_scales.rearrange("e g (q r) n -> r q (e g) n", r=4)
+        for r in range(4):
+            nc.sync.dma_start(w_scale_sb[r:P:32, :, :].bitcast(I32), scale_rows[r].bitcast(I32))
+        w_code_sb = keep.tile([P, E * PASSES, 4 * N], U8, name="w_code_sb", align_bytes=64)
+        nc.sync.dma_start(w_code_sb[:], w_words.rearrange("e g p n r -> p (e g) (n r)"))
+
+        sections = len(PAIR_PIECES) + 1
+        pairs = keep.tile([P, sections, T, 2], BF16, name="pairs")
+        nc.vector.memset(pairs[:, sections - 1, :, :], 0.0)
+        pair_words = pairs[:].rearrange("p i n v -> p (i n v)").bitcast(U32)
+        planes = keep.tile([P, 2, T], BF16, name="planes")
+        plain = keep.tile([P, 2, T, 2], BF16, name="plain")
+        grouped = [keep.tile([P, T, 4], BF16, name="grouped%d" % g, align_bytes=64) for g in range(PASSES)]
+        x_code = [keep.tile([P, T], U32, name="x_code%d" % g, align_bytes=64) for g in range(PASSES)]
+        x_scale = [keep.tile([P, T], U8, name="x_scale%d" % g, align_bytes=64) for g in range(PASSES)]
+        acc = [psum.tile([P, C], F32, name="acc%d" % e) for e in range(E)]
+        y = [keep.tile([P, HALF], F32, name="y%d" % h) for h in range(2)]
+        window_out = keep.tile([P, T], F32, name="window_out")
+
+        def entries(h):
+            return lists[:, h * (HALF // 16):(h + 1) * (HALF // 16)]
+
+        def words_of(g, dtype):
+            return grouped[g][:].rearrange("p s t -> p (s t)").bitcast(dtype).rearrange("p (s u) -> p s u", u=2)
+
+        def round_on_gpsimd(out, in_):
+            nc.gpsimd.tensor_scalar(out=out, in0=in_, scalar1=1.0, scalar2=0.0, op0=MULT, op1=ADD)
+
+        round_on = {"vector": nc.vector.tensor_copy, "scalar": nc.scalar.copy, "gpsimd": round_on_gpsimd}
+
+        def cast_pairs(i):
+            section = sections - 2 - i
+            for engine, start, count in PAIR_CASTS[i]:
+                tokens = slice(start, start + count)
+                round_on[engine](
+                    out=pairs[:, section, tokens, :].rearrange("p (c i) v -> p c v i", i=4),
+                    in_=raw_pairs[i][:, :, tokens].rearrange("p v (c i) -> p c v i", i=4),
+                )
+
+        def gather_pairs(i):
+            g, u = PAIR_PIECES[i]
+            section = sections - 2 - i
+            if g == EARLY:
+                words = plain[:, u, :, :].rearrange("p s v -> p (s v)").bitcast(U32)
+            else:
+                words = words_of(LATE, U32)[:, :, u]
+            nc.vector.tensor_copy(
+                words[:, 0:T], pair_words[:, section * T:(section + 2) * T].indirect(lists[:, 0:T // 16])
+            )
+
+        def interleave_early(h):
+            slots = slice(h * HALF, (h + 1) * HALF)
+            nc.vector.tensor_copy(
+                out=words_of(EARLY, I32)[:, slots, :],
+                in_=plain[:].rearrange("p u s v -> p (u s v)").bitcast(I32).rearrange("p (u s) -> p s u", u=2)[:, slots, :],
+            )
+
+        def quantize(g, h):
+            slots = slice(h * HALF, (h + 1) * HALF)
+            nc.vector.quantize_mx(
+                out=x_code[g][:, slots].bitcast(FP8X4),
+                scales=x_scale[g][:, slots],
+                in_=grouped[g][:, slots, :].rearrange("p s t -> p (s t)"),
+            )
+
+        def multiply(e, g, start, stop):
+            slots = slice(e * C, (e + 1) * C)
+            nc.tensor.matmul_mx(
+                out=acc[e][:],
+                lhsT=w_code_sb[:, e * PASSES + g, :].bitcast(FP8X4),
+                lhsT_scale=w_scale_sb[:, e * PASSES + g, :],
+                rhs=x_code[g][:, slots].bitcast(FP8X4),
+                rhs_scale=x_scale[g][:, slots],
+                start=start,
+                stop=stop,
+            )
+
+        for i in range(len(PAIR_PIECES)):
+            cast_pairs(i)
+            gather_pairs(i)
+
+        round_on_gpsimd(planes[:, 0, 0:PLANE0_FOR_GPSIMD], raw_planes[:, 0, 0:PLANE0_FOR_GPSIMD])
+        nc.scalar.copy(out=planes[:, 0, PLANE0_FOR_GPSIMD:T], in_=raw_planes[:, 0, PLANE0_FOR_GPSIMD:T])
+        round_on_gpsimd(planes[:, 1, :], raw_planes[:, 1, :])
+
+        for h in range(2):
+            interleave_early(h)
+        for h in range(2):
+            quantize(EARLY, h)
+            for e in (2 * h, 2 * h + 1):
+                multiply(e, EARLY, True, False)
+
+        both_planes = planes[:].rearrange("p v n -> p (v n)")
+        for h in range(2):
+            for v in range(2):
+                window = both_planes if (h, v) == (1, 0) else planes[:, v, :]
+                nc.scalar.activation(
+                    grouped[LATE][:, h * HALF:(h + 1) * HALF, 2 * PLANE_PIECE[1] + v], window.indirect(entries(h)), COPY
+                )
+            quantize(LATE, h)
+
+        for e in range(E):
+            multiply(e, LATE, False, True)
+            nc.scalar.copy(out=y[e // 2][:, (e % 2) * C:(e % 2 + 1) * C], in_=acc[e][:])
+        for h in range(2):
+            nc.vector.tensor_copy(window_out[:].indirect(entries(h)), y[h][:])
+        nc.sync.dma_start(out, window_out[:])

@@ -26,7 +26,7 @@ PAIR_PIECES = ((LATE, 0), (EARLY, 0), (EARLY, 1))
 PLANE_PIECE = (LATE, 1)
 
 PAIR_CASTS = (
-    (("vector", 0, 176), ("scalar", 176, 80), ("vector", 256, 88), ("scalar", 344, 40), ("vector", 384, 88), ("scalar", 472, 40)),
+    (("vector", 0, 288), ("scalar", 288, 224)),
     (("scalar", 0, 384), ("gpsimd", 384, 128)),
     (("scalar", 0, 368), ("gpsimd", 368, 144)),
 )
@@ -44,8 +44,7 @@ def tile_routed_moe_kernel(tc, xT, w_words, w_scales, offs, out):
         raw_pairs = [keep.tile([P, 2, T], F32, name="raw_pairs%d" % i) for i in range(len(PAIR_PIECES))]
         raw_planes = keep.tile([P, 2, T], F32, name="raw_planes")
         first = x_view[PAIR_PIECES[0][0], PAIR_PIECES[0][1]]
-        for a, b in ((0, 256), (256, 384), (384, 512)):
-            nc.sync.dma_start(raw_pairs[0][:, :, a:b], first[:, :, a:b])
+        nc.sync.dma_start(raw_pairs[0][:], first)
         nc.sync.dma_start(lists[:], offs)
         for i in range(1, len(PAIR_PIECES)):
             nc.sync.dma_start(raw_pairs[i][:], x_view[PAIR_PIECES[i][0], PAIR_PIECES[i][1]])

@@ -27,10 +27,10 @@ PLANE_PIECE = (LATE, 1)
 
 PAIR_CASTS = (
     (("vector", 0, 288), ("scalar", 288, 224)),
-    (("scalar", 0, 384), ("gpsimd", 384, 128)),
-    (("scalar", 0, 368), ("gpsimd", 368, 144)),
+    (("scalar", 0, 352), ("gpsimd", 352, 160)),
+    (("scalar", 0, 320), ("gpsimd", 320, 192)),
 )
-PLANE0_FOR_GPSIMD = 304
+PLANE0_FOR_GPSIMD = 320
 
 
 def tile_routed_moe_kernel(tc, xT, w_words, w_scales, offs, out):

@@ -145,11 +145,6 @@ def tile_routed_moe_kernel(tc, xT, w_words, w_scales, offs, out):
 
         for h in range(2):
             interleave_early(h)
-        for h in range(2):
-            quantize(EARLY, h)
-            for e in (2 * h, 2 * h + 1):
-                multiply(e, EARLY, True, False)
-
         both_planes = planes[:].rearrange("p v n -> p (v n)")
         for h in range(2):
             for v in range(2):
@@ -157,11 +152,16 @@ def tile_routed_moe_kernel(tc, xT, w_words, w_scales, offs, out):
                 nc.scalar.activation(
                     grouped[LATE][:, h * HALF:(h + 1) * HALF, 2 * PLANE_PIECE[1] + v], window.indirect(entries(h)), COPY
                 )
-            quantize(LATE, h)
 
-        for e in range(E):
-            multiply(e, LATE, False, True)
-            nc.scalar.copy(out=y[e // 2][:, (e % 2) * C:(e % 2 + 1) * C], in_=acc[e][:])
+        for h in range(2):
+            quantize(EARLY, h)
+            for e in (2 * h, 2 * h + 1):
+                multiply(e, EARLY, True, False)
+            quantize(LATE, h)
+            for e in (2 * h, 2 * h + 1):
+                multiply(e, LATE, False, True)
+                nc.scalar.copy(out=y[h][:, (e % 2) * C:(e % 2 + 1) * C], in_=acc[e][:])
+
         for h in range(2):
             nc.vector.tensor_copy(window_out[:].indirect(entries(h)), y[h][:])
         nc.sync.dma_start(out, window_out[:])

import concourse.mybir as mybir

FLOPS = 2 * 1024 * 128 * 512

F32 = mybir.dt.float32
BF16 = mybir.dt.bfloat16
I32 = mybir.dt.int32
U32 = mybir.dt.uint32
U16 = mybir.dt.uint16
U8 = mybir.dt.uint8
FP8X4 = mybir.dt.float8_e4m3fn_x4
COPY = mybir.ActivationFunctionType.Copy
MULT = mybir.AluOpType.mult
ADD = mybir.AluOpType.add

P = 128
T = 512
E = 4
C = 128
N = 128
PASSES = 2
HALF = T // 2

EARLY, LATE = 1, 0
PAIR_PIECES = ((LATE, 0), (EARLY, 0), (EARLY, 1))
PLANE_PIECE = (LATE, 1)

PAIR_CASTS = (
    (("vector", 0, 288), ("scalar", 288, 224)),
    (("scalar", 0, 352), ("gpsimd", 352, 160)),
    (("scalar", 0, 320), ("gpsimd", 320, 192)),
)
PLANE0_FOR_GPSIMD = 320


def tile_routed_moe_kernel(tc, xT, w_words, w_scales, offs, out):
    nc = tc.nc
    with (
        tc.tile_pool(name="keep", bufs=1) as keep,
        tc.psum_pool(name="psum", bufs=1) as psum,
    ):
        lists = keep.tile([P, T // 16], U16, name="lists")
        x_view = xT.rearrange("(g p u v) n -> g u p v n", g=PASSES, p=P, u=2, v=2)
        raw_pairs = [keep.tile([P, 2, T], F32, name="raw_pairs%d" % i) for i in range(len(PAIR_PIECES))]
        raw_planes = keep.tile([P, 2, T], F32, name="raw_planes")
        first = x_view[PAIR_PIECES[0][0], PAIR_PIECES[0][1]]
        nc.sync.dma_start(raw_pairs[0][:], first)
        nc.sync.dma_start(lists[:], offs)
        for i in range(1, len(PAIR_PIECES)):
            nc.sync.dma_start(raw_pairs[i][:], x_view[PAIR_PIECES[i][0], PAIR_PIECES[i][1]])
        for v in range(2):
            nc.sync.dma_start(raw_planes[:, v, :], x_view[PLANE_PIECE[0], PLANE_PIECE[1]][:, v, :])

        warm_in = keep.tile([P, 1], F32, name="warm_in")
        warm_out = keep.tile([P, 1], F32, name="warm_out")
        nc.vector.memset(warm_in[:], 0.0)
        nc.scalar.copy(out=warm_out[:], in_=warm_in[:])

        w_scale_sb = keep.tile([P, E * PASSES, N], U8, name="w_scale_sb", align_bytes=64)
        nc.vector.memset(w_scale_sb[:].rearrange("p i n -> p (i n)").bitcast(I32), 0)
        scale_rows = w_scales.rearrange("e g (q r) n -> r q (e g) n", r=4)
        for r in range(4):
            nc.sync.dma_start(w_scale_sb[r:P:32, :, :].bitcast(I32), scale_rows[r].bitcast(I32))
        w_code_sb = keep.tile([P, E * PASSES, 4 * N], U8, name="w_code_sb", align_bytes=64)
        nc.sync.dma_start(w_code_sb[:], w_words.rearrange("e g p n r -> p (e g) (n r)"))

        sections = len(PAIR_PIECES) + 1
        pairs = keep.tile([P, sections, T, 2], BF16, name="pairs")
        nc.vector.memset(pairs[:, sections - 1, :, :], 0.0)
        pair_words = pairs[:].rearrange("p i n v -> p (i n v)").bitcast(U32)
        planes = keep.tile([P, 2, T], BF16, name="planes")
        plain = keep.tile([P, 2, T, 2], BF16, name="plain")
        grouped = [keep.tile([P, T, 4], BF16, name="grouped%d" % g, align_bytes=64) for g in range(PASSES)]
        x_code = [keep.tile([P, T], U32, name="x_code%d" % g, align_bytes=64) for g in range(PASSES)]
        x_scale = [keep.tile([P, T], U8, name="x_scale%d" % g, align_bytes=64) for g in range(PASSES)]
        acc = [psum.tile([P, C], F32, name="acc%d" % e) for e in range(E)]
        y = [keep.tile([P, HALF], F32, name="y%d" % h) for h in range(2)]
        window_out = keep.tile([P, T], F32, name="window_out")

        def entries(h):
            return lists[:, h * (HALF // 16):(h + 1) * (HALF // 16)]

        def words_of(g, dtype):
            return grouped[g][:].rearrange("p s t -> p (s t)").bitcast(dtype).rearrange("p (s u) -> p s u", u=2)

        def round_on_gpsimd(out, in_):
            nc.gpsimd.tensor_scalar(out=out, in0=in_, scalar1=1.0, scalar2=0.0, op0=MULT, op1=ADD)

        round_on = {"vector": nc.vector.tensor_copy, "scalar": nc.scalar.copy, "gpsimd": round_on_gpsimd}

        def cast_pairs(i):
            section = sections - 2 - i
            for engine, start, count in PAIR_CASTS[i]:
                tokens = slice(start, start + count)
                round_on[engine](
                    out=pairs[:, section, tokens, :].rearrange("p (c i) v -> p c v i", i=4),
                    in_=raw_pairs[i][:, :, tokens].rearrange("p v (c i) -> p c v i", i=4),
                )

        def gather_pairs(i):
            g, u = PAIR_PIECES[i]
            section = sections - 2 - i
            if g == EARLY:
                words = plain[:, u, :, :].rearrange("p s v -> p (s v)").bitcast(U32)
            else:
                words = words_of(LATE, U32)[:, :, u]
            nc.vector.tensor_copy(
                words[:, 0:T], pair_words[:, section * T:(section + 2) * T].indirect(lists[:, 0:T // 16])
            )

        def interleave_early(h):
            slots = slice(h * HALF, (h + 1) * HALF)
            nc.vector.tensor_copy(
                out=words_of(EARLY, I32)[:, slots, :],
                in_=plain[:].rearrange("p u s v -> p (u s v)").bitcast(I32).rearrange("p (u s) -> p s u", u=2)[:, slots, :],
            )

        def quantize(g, h):
            slots = slice(h * HALF, (h + 1) * HALF)
            nc.vector.quantize_mx(
                out=x_code[g][:, slots].bitcast(FP8X4),
                scales=x_scale[g][:, slots],
                in_=grouped[g][:, slots, :].rearrange("p s t -> p (s t)"),
            )

        def multiply(e, g, start, stop):
            slots = slice(e * C, (e + 1) * C)
            nc.tensor.matmul_mx(
                out=acc[e][:],
                lhsT=w_code_sb[:, e * PASSES + g, :].bitcast(FP8X4),
                lhsT_scale=w_scale_sb[:, e * PASSES + g, :],
                rhs=x_code[g][:, slots].bitcast(FP8X4),
                rhs_scale=x_scale[g][:, slots],
                start=start,
                stop=stop,
            )

        for i in range(len(PAIR_PIECES)):
            cast_pairs(i)
            gather_pairs(i)

        round_on_gpsimd(planes[:, 0, 0:PLANE0_FOR_GPSIMD], raw_planes[:, 0, 0:PLANE0_FOR_GPSIMD])
        nc.scalar.copy(out=planes[:, 0, PLANE0_FOR_GPSIMD:T], in_=raw_planes[:, 0, PLANE0_FOR_GPSIMD:T])
        round_on_gpsimd(planes[:, 1, :], raw_planes[:, 1, :])

        for h in range(2):
            interleave_early(h)
        both_planes = planes[:].rearrange("p v n -> p (v n)")
        for h in range(2):
            for v in range(2):
                window = both_planes if (h, v) == (1, 0) else planes[:, v, :]
                nc.scalar.activation(
                    grouped[LATE][:, h * HALF:(h + 1) * HALF, 2 * PLANE_PIECE[1] + v], window.indirect(entries(h)), COPY
                )

        for h in range(2):
            quantize(EARLY, h)
            for e in (2 * h, 2 * h + 1):
                multiply(e, EARLY, True, False)
            quantize(LATE, h)
            for e in (2 * h, 2 * h + 1):
                multiply(e, LATE, False, True)
                nc.scalar.copy(out=y[h][:, (e % 2) * C:(e % 2 + 1) * C], in_=acc[e][:])

        for h in range(2):
            nc.vector.tensor_copy(window_out[:].indirect(entries(h)), y[h][:])
        nc.sync.dma_start(out, window_out[:])
